import numpy as np
import ml_dtypes


def mxq(x, axis, fmt="e4m3"):
    dtype, down = {"e4m3": (ml_dtypes.float8_e4m3fn, 7), "e5m2": (ml_dtypes.float8_e5m2, 14)}[fmt]
    v = np.moveaxis(np.asarray(x, np.float32).astype(ml_dtypes.bfloat16).astype(np.float64), axis, -1)
    blocks = v.reshape(v.shape[:-1] + (-1, 32))
    amax = np.abs(blocks).max(-1, keepdims=True)
    byte = np.maximum(np.where(amax > 0, np.frexp(amax)[1] - 1 + 127, 0) - down, 1)
    scale = np.exp2(byte - 127.0)
    codes = (blocks / scale).astype(np.float32).astype(dtype).astype(np.float64)
    return np.moveaxis((codes * scale).reshape(v.shape), -1, axis)


WIDE = False


def mx_kscale(k):
    if not WIDE:
        return np.ones(k)
    levels = np.array([10, -10, 5, -5, 0])
    if k % 512:
        return np.exp2(np.random.permutation(np.resize(levels, k // 32))).repeat(32)
    a = np.empty((k // 512, 16))
    for p in range(k // 512):
        a[p, :8] = np.random.permutation(np.resize(levels, 8))
        for g in range(8):
            far = levels[np.abs(levels - a[p, g]) >= 10]
            a[p, g + 8] = far[np.random.randint(len(far))]
    return np.exp2(a.ravel()).repeat(32)


def f64(x):
    return np.asarray(x).astype(np.float64)


def striped(idx):
    return np.tile(idx.reshape(-1, 16).T, (8, 1)).astype(np.uint16)


def unstriped(offs):
    return offs[:16].T.reshape(-1).astype(np.int64)


E2M1 = np.array([0.0, 0.5, 1.0, 1.5, 2.0, 3.0, 4.0, 6.0, -0.0, -0.5, -1.0, -1.5, -2.0, -3.0, -4.0, -6.0])


def pack_weight(w, fmt):
    k, n = w.shape
    w = f64(np.asarray(w, np.float32).astype(ml_dtypes.bfloat16)).reshape(k // 32, 32, n)
    amax = np.abs(w).max(1)
    if fmt == "e4m3":
        byte = np.frexp(amax)[1] - 1 + 127 - 7
    else:
        mant, ex = np.frexp(amax / 6.0)
        byte = np.where(mant > 0.5, ex, ex - 1) + 127
    byte = np.clip(np.where(amax > 0, byte, 1), 1, 254)
    scaled = (w * np.exp2(127.0 - byte)[:, None, :]).reshape(k, n).astype(np.float32)
    by_word = np.ascontiguousarray(scaled.reshape(k // 512, 128, 4, n).transpose(0, 1, 3, 2))
    if fmt == "e4m3":
        words = by_word.astype(ml_dtypes.float8_e4m3fn).view(np.uint8)
    else:
        c = by_word.astype(ml_dtypes.float4_e2m1fn).view(np.uint8) & 0xF
        words = (c[..., 0::2] | (c[..., 1::2] << 4)).reshape(k // 512, 128, 2 * n)
    return np.ascontiguousarray(words), np.ascontiguousarray(byte.astype(np.uint8).reshape(k // 512, 16, n))


def unpack_weight(words, scales, fmt):
    g, _, n = scales.shape
    words = np.ascontiguousarray(words).reshape(g, 128, n, -1)
    if fmt == "e4m3":
        vals = words.view(ml_dtypes.float8_e4m3fn).astype(np.float64)
    else:
        nib = np.empty((g, 128, n, 4), np.uint8)
        nib[..., 0::2] = words & 0xF
        nib[..., 1::2] = words >> 4
        vals = E2M1[nib]
    vals = vals * np.repeat(np.exp2(scales.astype(np.float64) - 127.0), 8, axis=1)[..., None]
    return vals.transpose(0, 1, 3, 2).reshape(g * 512, n)


def pack_table(v):
    words, scales = pack_weight(v, "e4m3")
    return np.concatenate([words.reshape(words.shape[0], -1), scales.reshape(scales.shape[0], -1)], axis=1)


def unpack_table(tab):
    g, t = tab.shape[0], tab.shape[1] // 528
    return unpack_weight(tab[:, :512 * t].reshape(g, 128, t, 4), tab[:, 512 * t:].reshape(g, 16, t), "e4m3")


def silu(v):
    return v / (1.0 + np.exp(-np.maximum(v, -700.0)))


K, M, T, S = 1024, 256, 1024, 512


def setup_inputs():
    n = np.random.standard_normal
    s = mx_kscale(K)[:, None]
    return {
        "tab": pack_table(n((K, T)) * s),
        "w": (n((K, M)) / np.sqrt(K) / s).astype(np.float32),
        "b": (0.3 * n(256)).astype(np.float32),
        "offs": striped(np.random.permutation(T)[:S]),
    }


def reference(tab, w, b, offs):
    tab_ = unpack_table(tab)[:, unstriped(offs)]
    w_ = mxq(f64(w), 0, "e4m3")
    y = tab_.T @ w_
    return silu(y + f64(b)[None, :])

@@ -1,0 +1,123 @@
+from contextlib import ExitStack
+
+import concourse.mybir as mybir
+from concourse.masks import make_identity
+
+K, M, T, S = 1024, 256, 1024, 512
+FLOPS = 2 * S * M * K
+
+F32 = mybir.dt.float32
+BF16 = mybir.dt.bfloat16
+I32 = mybir.dt.int32
+U32 = mybir.dt.uint32
+U16 = mybir.dt.uint16
+U8 = mybir.dt.uint8
+X4 = mybir.dt.float8_e4m3fn_x4
+ADD = mybir.AluOpType.add
+SILU = mybir.ActivationFunctionType.Silu
+
+P = 128
+PASSES = K // 512
+TOKENS = 128
+HALF = 128
+
+
+def tile_list_tabw_tm_silu_kernel(tc, tab, w, b, offs, out):
+    nc = tc.nc
+    with ExitStack() as ctx:
+        keep = ctx.enter_context(tc.tile_pool(name="keep", bufs=1))
+        psum = ctx.enter_context(tc.psum_pool(name="psum", bufs=1))
+
+        offsets = keep.tile([P, S // 16], U16, name="offsets")
+        nc.sync.dma_start(offsets[:], offs)
+
+        scale_rows = keep.tile([P, T // 4], I32, name="scale_rows", align_bytes=64)
+        nc.vector.memset(scale_rows[:], 0)
+        for q in range(4):
+            first = 512 * T + 4 * q * T
+            nc.scalar.dma_start(
+                scale_rows[32 * q : 32 * q + 8, :],
+                tab[:, first : first + 4 * T].rearrange("a (r t) -> a r t", r=4).bitcast(I32),
+            )
+
+        one = keep.tile([P, 1], F32, name="one")
+        nc.vector.memset(one[:], 0.0)
+        warm = keep.tile([P, 1], F32, name="warm")
+        nc.scalar.activation(warm[:], one[:], SILU)
+
+        words = []
+        raw = []
+        for a in range(PASSES):
+            words_a = keep.tile([P, T], I32, name="words%d" % a, align_bytes=64)
+            nc.sync.dma_start(words_a[:], tab[a, 0 : 512 * T].rearrange("(p t) -> p t", p=P).bitcast(I32))
+            words.append(words_a)
+            raw_a = keep.tile([P, 4, M], F32, name="raw%d" % a, align_bytes=64)
+            nc.sync.dma_start(raw_a[:], w[512 * a : 512 * a + 512, :].rearrange("(p j) n -> p j n", j=4))
+            raw.append(raw_a)
+
+        b_col = keep.tile([P, M // P], F32, name="b_col")
+        with nc.allow_non_contiguous_dma(reason="a bias of 1 KiB, one element to a partition"):
+            nc.scalar.dma_start(b_col[:], b.rearrange("(h p) -> p h", p=P))
+        identity = keep.tile([P, P], F32, name="identity")
+        make_identity(nc, identity[:])
+        b_bank = psum.tile([P, M], F32, name="b_bank")
+        for h in range(M // P):
+            nc.tensor.transpose(b_bank[:, P * h : P * h + P], b_col[:, h : h + 1].to_broadcast([P, P]), identity[:])
+        b_rows = keep.tile([P, M], F32, name="b_rows")
+        nc.scalar.copy(b_rows[:], b_bank[:])
+
+        picked_scales = keep.tile([P, S], U8, name="picked_scales", align_bytes=64)
+        picked = keep.tile([P, PASSES, S], U32, name="picked", align_bytes=64)
+        w_codes = keep.tile([P, PASSES, M], U32, name="w_codes", align_bytes=64)
+        w_scales = keep.tile([P, PASSES, M], U8, name="w_scales", align_bytes=64)
+
+        def gather_words(a, j0, j1):
+            nc.vector.tensor_copy(picked[:, a, j0:j1], words[a][:].bitcast(U32).indirect(offsets[:, j0 // 16 : j1 // 16]))
+
+        def interleave(a, h, engine_copy):
+            grouped = keep.tile([P, HALF, 4], BF16, name="grouped%d%d" % (a, h), align_bytes=64)
+            engine_copy(grouped[:], raw[a][:, :, HALF * h : HALF * h + HALF].rearrange("p j n -> p n j"))
+            return grouped
+
+        def quantize(a, h, grouped):
+            cols = slice(HALF * h, HALF * h + HALF)
+            nc.vector.quantize_mx(
+                out=w_codes[:, a, cols].bitcast(X4),
+                scales=w_scales[:, a, cols],
+                in_=grouped[:].rearrange("p n j -> p (n j)"),
+            )
+
+        nc.vector.tensor_copy(picked_scales[:], scale_rows[:].bitcast(U8).indirect(offsets[:]))
+        gather_words(0, 0, S)
+        left = interleave(0, 0, nc.scalar.copy)
+        right = interleave(0, 1, nc.vector.tensor_copy)
+        quantize(0, 0, left)
+        quantize(0, 1, right)
+        gather_words(1, 0, S)
+        left = interleave(1, 0, nc.scalar.copy)
+        right = interleave(1, 1, nc.vector.tensor_copy)
+        quantize(1, 1, right)
+        quantize(1, 0, left)
+
+        banks = []
+        for t in range(S // TOKENS):
+            bank = psum.tile([P, M], F32, name="bank%d" % t)
+            banks.append(bank)
+        for a in range(PASSES):
+            for t in range(S // TOKENS):
+                tokens = slice(TOKENS * t, TOKENS * t + TOKENS)
+                nc.tensor.matmul_mx(
+                    out=banks[t][:],
+                    lhsT=picked[:, a, tokens].bitcast(X4),
+                    lhsT_scale=picked_scales[4 * a : P, tokens],
+                    rhs=w_codes[:, a, :].bitcast(X4),
+                    rhs_scale=w_scales[:, a, :],
+                    start=(a == 0),
+                    stop=(a == PASSES - 1),
+                )
+        for t in range(S // TOKENS):
+            y = keep.tile([P, M], F32, name="y%d" % t)
+            nc.vector.tensor_tensor(y[:], banks[t][:], b_rows[:], ADD)
+            result = keep.tile([P, M], F32, name="result%d" % t)
+            nc.scalar.activation(result[:], y[:], SILU)
+            nc.sync.dma_start(out[TOKENS * t : TOKENS * t + TOKENS, :], result[:])

@@ -19,7 +19,7 @@ SILU = mybir.ActivationFunctionType.Silu
 P = 128
 PASSES = K // 512
 TOKENS = 128
-HALF = 128
+HALF = M // 2
 
 
 def tile_list_tabw_tm_silu_kernel(tc, tab, w, b, offs, out):
@@ -31,33 +31,48 @@ def tile_list_tabw_tm_silu_kernel(tc, tab, w, b, offs, out):
         offsets = keep.tile([P, S // 16], U16, name="offsets")
         nc.sync.dma_start(offsets[:], offs)
 
-        scale_rows = keep.tile([P, T // 4], I32, name="scale_rows", align_bytes=64)
-        nc.vector.memset(scale_rows[:], 0)
-        for q in range(4):
-            first = 512 * T + 4 * q * T
-            nc.scalar.dma_start(
-                scale_rows[32 * q : 32 * q + 8, :],
-                tab[:, first : first + 4 * T].rearrange("a (r t) -> a r t", r=4).bitcast(I32),
-            )
-
-        one = keep.tile([P, 1], F32, name="one")
-        nc.vector.memset(one[:], 0.0)
-        warm = keep.tile([P, 1], F32, name="warm")
-        nc.scalar.activation(warm[:], one[:], SILU)
-
-        words = []
-        raw = []
-        for a in range(PASSES):
-            words_a = keep.tile([P, T], I32, name="words%d" % a, align_bytes=64)
-            nc.sync.dma_start(words_a[:], tab[a, 0 : 512 * T].rearrange("(p t) -> p t", p=P).bitcast(I32))
-            words.append(words_a)
-            raw_a = keep.tile([P, 4, M], F32, name="raw%d" % a, align_bytes=64)
-            nc.sync.dma_start(raw_a[:], w[512 * a : 512 * a + 512, :].rearrange("(p j) n -> p j n", j=4))
-            raw.append(raw_a)
-
         b_col = keep.tile([P, M // P], F32, name="b_col")
         with nc.allow_non_contiguous_dma(reason="a bias of 1 KiB, one element to a partition"):
             nc.scalar.dma_start(b_col[:], b.rearrange("(h p) -> p h", p=P))
+
+        front = keep.tile([P, T // 4 + T], I32, name="front", align_bytes=64)
+        nc.gpsimd.memset(front[:, 0 : T // 4 + 8], 0)
+        scale_rows = front[:, 0 : T // 4]
+        one = keep.tile([P, 1], F32, name="one")
+        nc.vector.memset(one[:], 0.0)
+
+        def load_scales():
+            for q in range(4):
+                first = 512 * T + 4 * q * T
+                nc.sync.dma_start(
+                    front[32 * q : 32 * q + 8, 0 : T // 4],
+                    tab[:, first : first + 4 * T].rearrange("a (r t) -> a r t", r=4).bitcast(I32),
+                )
+
+        def load_words(a):
+            words_a = front[:, T // 4 : T // 4 + T]
+            if a == 1:
+                words1 = keep.tile([P, T], I32, name="words1", align_bytes=64)
+                words_a = words1[:]
+            nc.sync.dma_start(words_a, tab[a, 0 : 512 * T].rearrange("(p t) -> p t", p=P).bitcast(I32))
+            return words_a
+
+        def load_weights(a):
+            raw_a = keep.tile([P, 4, M], F32, name="raw%d" % a, align_bytes=64)
+            nc.sync.dma_start(raw_a[:], w[512 * a : 512 * a + 512, :].rearrange("(p j) n -> p j n", j=4))
+            return raw_a
+
+        words, raw = {}, {}
+
+        load_scales()
+        words[0] = load_words(0)
+        raw[0] = load_weights(0)
+        raw[1] = load_weights(1)
+        words[1] = load_words(1)
+
+        warm = keep.tile([P, 1], F32, name="warm")
+        nc.scalar.activation(warm[:], one[:], SILU)
+
         identity = keep.tile([P, P], F32, name="identity")
         make_identity(nc, identity[:])
         b_bank = psum.tile([P, M], F32, name="b_bank")
@@ -72,52 +87,70 @@ def tile_list_tabw_tm_silu_kernel(tc, tab, w, b, offs, out):
         w_scales = keep.tile([P, PASSES, M], U8, name="w_scales", align_bytes=64)
 
         def gather_words(a, j0, j1):
-            nc.vector.tensor_copy(picked[:, a, j0:j1], words[a][:].bitcast(U32).indirect(offsets[:, j0 // 16 : j1 // 16]))
+            nc.vector.tensor_copy(picked[:, a, j0:j1], words[a].bitcast(U32).indirect(offsets[:, j0 // 16 : j1 // 16]))
 
-        def interleave(a, h, engine_copy):
-            grouped = keep.tile([P, HALF, 4], BF16, name="grouped%d%d" % (a, h), align_bytes=64)
-            engine_copy(grouped[:], raw[a][:, :, HALF * h : HALF * h + HALF].rearrange("p j n -> p n j"))
-            return grouped
+        def gather_scales():
+            nc.vector.tensor_copy(picked_scales[:], scale_rows.bitcast(U8).indirect(offsets[:]))
 
-        def quantize(a, h, grouped):
-            cols = slice(HALF * h, HALF * h + HALF)
+        grouped = {}
+
+        def interleave(a, n0, n1, engine_copy):
+            g = keep.tile([P, n1 - n0, 4], BF16, name="grouped%d_%d" % (a, n0), align_bytes=64)
+            engine_copy(g[:], raw[a][:, :, n0:n1].rearrange("p j n -> p n j"))
+            grouped[a, n0, n1] = g
+
+        def quantize(a, n0, n1):
             nc.vector.quantize_mx(
-                out=w_codes[:, a, cols].bitcast(X4),
-                scales=w_scales[:, a, cols],
-                in_=grouped[:].rearrange("p n j -> p (n j)"),
+                out=w_codes[:, a, n0:n1].bitcast(X4),
+                scales=w_scales[:, a, n0:n1],
+                in_=grouped[a, n0, n1][:].rearrange("p n j -> p (n j)"),
             )
-
-        nc.vector.tensor_copy(picked_scales[:], scale_rows[:].bitcast(U8).indirect(offsets[:]))
-        gather_words(0, 0, S)
-        left = interleave(0, 0, nc.scalar.copy)
-        right = interleave(0, 1, nc.vector.tensor_copy)
-        quantize(0, 0, left)
-        quantize(0, 1, right)
-        gather_words(1, 0, S)
-        left = interleave(1, 0, nc.scalar.copy)
-        right = interleave(1, 1, nc.vector.tensor_copy)
-        quantize(1, 1, right)
-        quantize(1, 0, left)
 
         banks = []
         for t in range(S // TOKENS):
             bank = psum.tile([P, M], F32, name="bank%d" % t)
             banks.append(bank)
-        for a in range(PASSES):
-            for t in range(S // TOKENS):
-                tokens = slice(TOKENS * t, TOKENS * t + TOKENS)
-                nc.tensor.matmul_mx(
-                    out=banks[t][:],
-                    lhsT=picked[:, a, tokens].bitcast(X4),
-                    lhsT_scale=picked_scales[4 * a : P, tokens],
-                    rhs=w_codes[:, a, :].bitcast(X4),
-                    rhs_scale=w_scales[:, a, :],
-                    start=(a == 0),
-                    stop=(a == PASSES - 1),
-                )
-        for t in range(S // TOKENS):
+
+        def multiply(a, t):
+            tokens = slice(TOKENS * t, TOKENS * t + TOKENS)
+            nc.tensor.matmul_mx(
+                out=banks[t][:],
+                lhsT=picked[:, a, tokens].bitcast(X4),
+                lhsT_scale=picked_scales[4 * a : P, tokens],
+                rhs=w_codes[:, a, :].bitcast(X4),
+                rhs_scale=w_scales[:, a, :],
+                start=(a == 0),
+                stop=(a == PASSES - 1),
+            )
+
+        def finish(t):
             y = keep.tile([P, M], F32, name="y%d" % t)
             nc.vector.tensor_tensor(y[:], banks[t][:], b_rows[:], ADD)
             result = keep.tile([P, M], F32, name="result%d" % t)
             nc.scalar.activation(result[:], y[:], SILU)
             nc.sync.dma_start(out[TOKENS * t : TOKENS * t + TOKENS, :], result[:])
+
+        gather_scales()
+        gather_words(0, 0, S)
+        interleave(0, 0, HALF, nc.scalar.copy)
+        interleave(0, HALF, M, nc.vector.tensor_copy)
+        quantize(0, 0, HALF)
+        quantize(0, HALF, M)
+        for t in range(4):
+            multiply(0, t)
+        interleave(1, 0, HALF, nc.scalar.copy)
+        interleave(1, HALF, M, nc.vector.tensor_copy)
+        quantize(1, 0, HALF)
+        quantize(1, HALF, M)
+        gather_words(1, 0, 128)
+        multiply(1, 0)
+        gather_words(1, 128, 256)
+        multiply(1, 1)
+        finish(0)
+        gather_words(1, 256, 384)
+        multiply(1, 2)
+        finish(1)
+        gather_words(1, 384, 512)
+        multiply(1, 3)
+        finish(2)
+        finish(3)

@@ -33,11 +33,12 @@ def tile_list_tabw_tm_silu_kernel(tc, tab, w, b, offs, out):
 
         b_col = keep.tile([P, M // P], F32, name="b_col")
         with nc.allow_non_contiguous_dma(reason="a bias of 1 KiB, one element to a partition"):
-            nc.scalar.dma_start(b_col[:], b.rearrange("(h p) -> p h", p=P))
-
-        front = keep.tile([P, T // 4 + T], I32, name="front", align_bytes=64)
-        nc.gpsimd.memset(front[:, 0 : T // 4 + 8], 0)
-        scale_rows = front[:, 0 : T // 4]
+            nc.sync.dma_start(b_col[:], b.rearrange("(h p) -> p h", p=P))
+        tables = keep.tile([P, T // 4 + PASSES * T], I32, name="tables", align_bytes=64)
+        nc.gpsimd.memset(tables[:, 0 : T // 4], 0)
+        nc.gpsimd.memset(tables[:, T // 4 :].rearrange("p (a t) -> p a t", t=T)[:, :, 0:8], 0)
+        weights = keep.tile([P, PASSES, 4 * M], F32, name="weights", align_bytes=64)
+        nc.vector.memset(weights[:, :, 0:8], 0.0)
         one = keep.tile([P, 1], F32, name="one")
         nc.vector.memset(one[:], 0.0)
 
@@ -45,30 +46,23 @@ def tile_list_tabw_tm_silu_kernel(tc, tab, w, b, offs, out):
             for q in range(4):
                 first = 512 * T + 4 * q * T
                 nc.sync.dma_start(
-                    front[32 * q : 32 * q + 8, 0 : T // 4],
+                    tables[32 * q : 32 * q + 8, 0 : T // 4],
                     tab[:, first : first + 4 * T].rearrange("a (r t) -> a r t", r=4).bitcast(I32),
                 )
 
+        words = [tables[:, T // 4 + a * T : T // 4 + a * T + T] for a in range(PASSES)]
+
         def load_words(a):
-            words_a = front[:, T // 4 : T // 4 + T]
-            if a == 1:
-                words1 = keep.tile([P, T], I32, name="words1", align_bytes=64)
-                words_a = words1[:]
-            nc.sync.dma_start(words_a, tab[a, 0 : 512 * T].rearrange("(p t) -> p t", p=P).bitcast(I32))
-            return words_a
+            nc.sync.dma_start(words[a], tab[a, 0 : 512 * T].rearrange("(p t) -> p t", p=P).bitcast(I32))
 
         def load_weights(a):
-            raw_a = keep.tile([P, 4, M], F32, name="raw%d" % a, align_bytes=64)
-            nc.sync.dma_start(raw_a[:], w[512 * a : 512 * a + 512, :].rearrange("(p j) n -> p j n", j=4))
-            return raw_a
-
-        words, raw = {}, {}
+            nc.sync.dma_start(weights[:, a, :], w[512 * a : 512 * a + 512, :].rearrange("(p j) n -> p (j n)", j=4))
 
         load_scales()
-        words[0] = load_words(0)
-        raw[0] = load_weights(0)
-        raw[1] = load_weights(1)
-        words[1] = load_words(1)
+        load_words(0)
+        load_weights(0)
+        load_words(1)
+        load_weights(1)
 
         warm = keep.tile([P, 1], F32, name="warm")
         nc.scalar.activation(warm[:], one[:], SILU)
@@ -87,23 +81,28 @@ def tile_list_tabw_tm_silu_kernel(tc, tab, w, b, offs, out):
         w_scales = keep.tile([P, PASSES, M], U8, name="w_scales", align_bytes=64)
 
         def gather_words(a, j0, j1):
-            nc.vector.tensor_copy(picked[:, a, j0:j1], words[a].bitcast(U32).indirect(offsets[:, j0 // 16 : j1 // 16]))
+            nc.vector.tensor_copy(
+                picked[:, a, j0:j1],
+                words[a].bitcast(U32).indirect(offsets[:, j0 // 16 : j1 // 16]),
+            )
 
         def gather_scales():
-            nc.vector.tensor_copy(picked_scales[:], scale_rows.bitcast(U8).indirect(offsets[:]))
+            nc.vector.tensor_copy(picked_scales[:], tables[:, 0 : T // 4].bitcast(U8).indirect(offsets[:]))
 
         grouped = {}
 
         def interleave(a, n0, n1, engine_copy):
-            g = keep.tile([P, n1 - n0, 4], BF16, name="grouped%d_%d" % (a, n0), align_bytes=64)
-            engine_copy(g[:], raw[a][:, :, n0:n1].rearrange("p j n -> p n j"))
-            grouped[a, n0, n1] = g
+            if a not in grouped:
+                g = keep.tile([P, M, 4], BF16, name="grouped%d" % a, align_bytes=64)
+                grouped[a] = g
+            rows = weights[:, a, :].rearrange("p (j n) -> p n j", j=4)
+            engine_copy(grouped[a][:, n0:n1, :], rows[:, n0:n1, :])
 
         def quantize(a, n0, n1):
             nc.vector.quantize_mx(
                 out=w_codes[:, a, n0:n1].bitcast(X4),
                 scales=w_scales[:, a, n0:n1],
-                in_=grouped[a, n0, n1][:].rearrange("p n j -> p (n j)"),
+                in_=grouped[a][:, n0:n1, :].rearrange("p n j -> p (n j)"),
             )
 
         banks = []
@@ -134,23 +133,14 @@ def tile_list_tabw_tm_silu_kernel(tc, tab, w, b, offs, out):
         gather_words(0, 0, S)
         interleave(0, 0, HALF, nc.scalar.copy)
         interleave(0, HALF, M, nc.vector.tensor_copy)
-        quantize(0, 0, HALF)
-        quantize(0, HALF, M)
+        quantize(0, 0, M)
         for t in range(4):
             multiply(0, t)
-        interleave(1, 0, HALF, nc.scalar.copy)
-        interleave(1, HALF, M, nc.vector.tensor_copy)
-        quantize(1, 0, HALF)
-        quantize(1, HALF, M)
-        gather_words(1, 0, 128)
-        multiply(1, 0)
-        gather_words(1, 128, 256)
-        multiply(1, 1)
-        finish(0)
-        gather_words(1, 256, 384)
-        multiply(1, 2)
-        finish(1)
-        gather_words(1, 384, 512)
-        multiply(1, 3)
-        finish(2)
-        finish(3)
+        gather_words(1, 0, 384)
+        interleave(1, 0, 96, nc.scalar.copy)
+        interleave(1, 96, M, nc.vector.tensor_copy)
+        quantize(1, 0, M)
+        gather_words(1, 384, S)
+        for t in range(4):
+            multiply(1, t)
+            finish(t)

@@ -31,12 +31,11 @@ def tile_list_tabw_tm_silu_kernel(tc, tab, w, b, offs, out):
         offsets = keep.tile([P, S // 16], U16, name="offsets")
         nc.sync.dma_start(offsets[:], offs)
 
-        b_col = keep.tile([P, M // P], F32, name="b_col")
-        with nc.allow_non_contiguous_dma(reason="a bias of 1 KiB, one element to a partition"):
-            nc.sync.dma_start(b_col[:], b.rearrange("(h p) -> p h", p=P))
+        b_pairs = keep.tile([P, M // P], F32, name="b_pairs")
+        nc.sync.dma_start(b_pairs[:], b.rearrange("(p h) -> p h", h=M // P))
         tables = keep.tile([P, T // 4 + PASSES * T], I32, name="tables", align_bytes=64)
         nc.gpsimd.memset(tables[:, 0 : T // 4], 0)
-        nc.gpsimd.memset(tables[:, T // 4 :].rearrange("p (a t) -> p a t", t=T)[:, :, 0:8], 0)
+        nc.gpsimd.memset(tables[:, T // 4 + T : T // 4 + T + 8], 0)
         weights = keep.tile([P, PASSES, 4 * M], F32, name="weights", align_bytes=64)
         nc.vector.memset(weights[:, :, 0:8], 0.0)
         one = keep.tile([P, 1], F32, name="one")
@@ -58,8 +57,8 @@ def tile_list_tabw_tm_silu_kernel(tc, tab, w, b, offs, out):
         def load_weights(a):
             nc.sync.dma_start(weights[:, a, :], w[512 * a : 512 * a + 512, :].rearrange("(p j) n -> p (j n)", j=4))
 
-        load_scales()
         load_words(0)
+        load_scales()
         load_weights(0)
         load_words(1)
         load_weights(1)
@@ -69,11 +68,11 @@ def tile_list_tabw_tm_silu_kernel(tc, tab, w, b, offs, out):
 
         identity = keep.tile([P, P], F32, name="identity")
         make_identity(nc, identity[:])
-        b_bank = psum.tile([P, M], F32, name="b_bank")
+        b_bank = psum.tile([P, M // P, P], F32, name="b_bank")
         for h in range(M // P):
-            nc.tensor.transpose(b_bank[:, P * h : P * h + P], b_col[:, h : h + 1].to_broadcast([P, P]), identity[:])
+            nc.tensor.transpose(b_bank[:, h, :], b_pairs[:, h : h + 1].to_broadcast([P, P]), identity[:])
         b_rows = keep.tile([P, M], F32, name="b_rows")
-        nc.scalar.copy(b_rows[:], b_bank[:])
+        nc.scalar.copy(b_rows[:].rearrange("p (n h) -> p n h", h=M // P), b_bank[:].rearrange("p h n -> p n h"))
 
         picked_scales = keep.tile([P, S], U8, name="picked_scales", align_bytes=64)
         picked = keep.tile([P, PASSES, S], U32, name="picked", align_bytes=64)
@@ -129,10 +128,9 @@ def tile_list_tabw_tm_silu_kernel(tc, tab, w, b, offs, out):
             nc.scalar.activation(result[:], y[:], SILU)
             nc.sync.dma_start(out[TOKENS * t : TOKENS * t + TOKENS, :], result[:])
 
-        gather_scales()
         gather_words(0, 0, S)
-        interleave(0, 0, HALF, nc.scalar.copy)
-        interleave(0, HALF, M, nc.vector.tensor_copy)
+        gather_scales()
+        interleave(0, 0, M, nc.scalar.copy)
         quantize(0, 0, M)
         for t in range(4):
             multiply(0, t)

from contextlib import ExitStack

import concourse.mybir as mybir
from concourse.masks import make_identity

K, M, T, S = 1024, 256, 1024, 512
FLOPS = 2 * S * M * K

F32 = mybir.dt.float32
BF16 = mybir.dt.bfloat16
I32 = mybir.dt.int32
U32 = mybir.dt.uint32
U16 = mybir.dt.uint16
U8 = mybir.dt.uint8
X4 = mybir.dt.float8_e4m3fn_x4
ADD = mybir.AluOpType.add
SILU = mybir.ActivationFunctionType.Silu

P = 128
PASSES = K // 512
TOKENS = 128
HALF = M // 2


def tile_list_tabw_tm_silu_kernel(tc, tab, w, b, offs, out):
    nc = tc.nc
    with ExitStack() as ctx:
        keep = ctx.enter_context(tc.tile_pool(name="keep", bufs=1))
        psum = ctx.enter_context(tc.psum_pool(name="psum", bufs=1))

        offsets = keep.tile([P, S // 16], U16, name="offsets")
        nc.sync.dma_start(offsets[:], offs)

        b_pairs = keep.tile([P, M // P], F32, name="b_pairs")
        nc.sync.dma_start(b_pairs[:], b.rearrange("(p h) -> p h", h=M // P))
        tables = keep.tile([P, T // 4 + PASSES * T], I32, name="tables", align_bytes=64)
        nc.gpsimd.memset(tables[:, 0 : T // 4], 0)
        nc.gpsimd.memset(tables[:, T // 4 + T : T // 4 + T + 8], 0)
        weights = keep.tile([P, PASSES, 4 * M], F32, name="weights", align_bytes=64)
        nc.vector.memset(weights[:, :, 0:8], 0.0)
        one = keep.tile([P, 1], F32, name="one")
        nc.vector.memset(one[:], 0.0)

        def load_scales():
            for q in range(4):
                first = 512 * T + 4 * q * T
                nc.sync.dma_start(
                    tables[32 * q : 32 * q + 8, 0 : T // 4],
                    tab[:, first : first + 4 * T].rearrange("a (r t) -> a r t", r=4).bitcast(I32),
                )

        words = [tables[:, T // 4 + a * T : T // 4 + a * T + T] for a in range(PASSES)]

        def load_words(a):
            nc.sync.dma_start(words[a], tab[a, 0 : 512 * T].rearrange("(p t) -> p t", p=P).bitcast(I32))

        def load_weights(a):
            nc.sync.dma_start(weights[:, a, :], w[512 * a : 512 * a + 512, :].rearrange("(p j) n -> p (j n)", j=4))

        load_words(0)
        load_scales()
        load_weights(0)
        load_words(1)
        load_weights(1)

        warm = keep.tile([P, 1], F32, name="warm")
        nc.scalar.activation(warm[:], one[:], SILU)

        identity = keep.tile([P, P], F32, name="identity")
        make_identity(nc, identity[:])
        b_bank = psum.tile([P, M // P, P], F32, name="b_bank")
        for h in range(M // P):
            nc.tensor.transpose(b_bank[:, h, :], b_pairs[:, h : h + 1].to_broadcast([P, P]), identity[:])
        b_rows = keep.tile([P, M], F32, name="b_rows")
        nc.scalar.copy(b_rows[:].rearrange("p (n h) -> p n h", h=M // P), b_bank[:].rearrange("p h n -> p n h"))

        picked_scales = keep.tile([P, S], U8, name="picked_scales", align_bytes=64)
        picked = keep.tile([P, PASSES, S], U32, name="picked", align_bytes=64)
        w_codes = keep.tile([P, PASSES, M], U32, name="w_codes", align_bytes=64)
        w_scales = keep.tile([P, PASSES, M], U8, name="w_scales", align_bytes=64)

        def gather_words(a, j0, j1):
            nc.vector.tensor_copy(
                picked[:, a, j0:j1],
                words[a].bitcast(U32).indirect(offsets[:, j0 // 16 : j1 // 16]),
            )

        def gather_scales():
            nc.vector.tensor_copy(picked_scales[:], tables[:, 0 : T // 4].bitcast(U8).indirect(offsets[:]))

        grouped = {}

        def interleave(a, n0, n1, engine_copy):
            if a not in grouped:
                g = keep.tile([P, M, 4], BF16, name="grouped%d" % a, align_bytes=64)
                grouped[a] = g
            rows = weights[:, a, :].rearrange("p (j n) -> p n j", j=4)
            engine_copy(grouped[a][:, n0:n1, :], rows[:, n0:n1, :])

        def quantize(a, n0, n1):
            nc.vector.quantize_mx(
                out=w_codes[:, a, n0:n1].bitcast(X4),
                scales=w_scales[:, a, n0:n1],
                in_=grouped[a][:, n0:n1, :].rearrange("p n j -> p (n j)"),
            )

        banks = []
        for t in range(S // TOKENS):
            bank = psum.tile([P, M], F32, name="bank%d" % t)
            banks.append(bank)

        def multiply(a, t):
            tokens = slice(TOKENS * t, TOKENS * t + TOKENS)
            nc.tensor.matmul_mx(
                out=banks[t][:],
                lhsT=picked[:, a, tokens].bitcast(X4),
                lhsT_scale=picked_scales[4 * a : P, tokens],
                rhs=w_codes[:, a, :].bitcast(X4),
                rhs_scale=w_scales[:, a, :],
                start=(a == 0),
                stop=(a == PASSES - 1),
            )

        def finish(t):
            y = keep.tile([P, M], F32, name="y%d" % t)
            nc.vector.tensor_tensor(y[:], banks[t][:], b_rows[:], ADD)
            result = keep.tile([P, M], F32, name="result%d" % t)
            nc.scalar.activation(result[:], y[:], SILU)
            nc.sync.dma_start(out[TOKENS * t : TOKENS * t + TOKENS, :], result[:])

        gather_words(0, 0, S)
        gather_scales()
        interleave(0, 0, M, nc.scalar.copy)
        quantize(0, 0, M)
        for t in range(4):
            multiply(0, t)
        gather_words(1, 0, 384)
        interleave(1, 0, 96, nc.scalar.copy)
        interleave(1, 96, M, nc.vector.tensor_copy)
        quantize(1, 0, M)
        gather_words(1, 384, S)
        for t in range(4):
            multiply(1, t)
            finish(t)
